import numpy as np
import ml_dtypes


def mxq(x, axis, fmt="e4m3"):
    dtype, down = {"e4m3": (ml_dtypes.float8_e4m3fn, 7), "e5m2": (ml_dtypes.float8_e5m2, 14)}[fmt]
    v = np.moveaxis(np.asarray(x, np.float32).astype(ml_dtypes.bfloat16).astype(np.float64), axis, -1)
    blocks = v.reshape(v.shape[:-1] + (-1, 32))
    amax = np.abs(blocks).max(-1, keepdims=True)
    byte = np.maximum(np.where(amax > 0, np.frexp(amax)[1] - 1 + 127, 0) - down, 1)
    scale = np.exp2(byte - 127.0)
    codes = (blocks / scale).astype(np.float32).astype(dtype).astype(np.float64)
    return np.moveaxis((codes * scale).reshape(v.shape), -1, axis)


WIDE = False


def mx_kscale(k):
    if not WIDE:
        return np.ones(k)
    levels = np.array([10, -10, 5, -5, 0])
    if k % 512:
        return np.exp2(np.random.permutation(np.resize(levels, k // 32))).repeat(32)
    a = np.empty((k // 512, 16))
    for p in range(k // 512):
        a[p, :8] = np.random.permutation(np.resize(levels, 8))
        for g in range(8):
            far = levels[np.abs(levels - a[p, g]) >= 10]
            a[p, g + 8] = far[np.random.randint(len(far))]
    return np.exp2(a.ravel()).repeat(32)


def f64(x):
    return np.asarray(x).astype(np.float64)


def striped(idx):
    return np.tile(idx.reshape(-1, 16).T, (8, 1)).astype(np.uint16)


def unstriped(offs):
    return offs[:16].T.reshape(-1).astype(np.int64)


def pack_weight(w):
    k, n = w.shape
    w = f64(np.asarray(w, np.float32).astype(ml_dtypes.bfloat16)).reshape(k // 32, 32, n)
    amax = np.abs(w).max(1)
    byte = np.clip(np.where(amax > 0, np.frexp(amax)[1] - 1 + 127 - 7, 1), 1, 254)
    scaled = (w * np.exp2(127.0 - byte)[:, None, :]).reshape(k, n).astype(np.float32)
    words = np.ascontiguousarray(scaled.reshape(k // 512, 128, 4, n).transpose(0, 1, 3, 2)).astype(ml_dtypes.float8_e4m3fn).view(np.uint8)
    return words, np.ascontiguousarray(byte.astype(np.uint8).reshape(k // 512, 16, n))


def unpack_weight(words, scales):
    g, p, n, _ = words.shape
    vals = np.ascontiguousarray(words).view(ml_dtypes.float8_e4m3fn).astype(np.float64) * np.repeat(np.exp2(scales.astype(np.float64) - 127.0), 8, axis=1)[..., None]
    return vals.transpose(0, 1, 3, 2).reshape(g * 512, n)


K, T, S, H, N = 1024, 1024, 512, 512, 128


def setup_inputs():
    n = np.random.standard_normal
    s = mx_kscale(K)[:, None]
    u = mx_kscale(H)
    packed_xT = pack_weight(n((K, T)) * s)
    return {
        "x_words": packed_xT[0],
        "x_scales": packed_xT[1],
        "w1": (n((K, H)) / np.sqrt(K) / s).astype(np.float32),
        "w2": (n((K, H)) / np.sqrt(K) / s).astype(np.float32),
        "w3": (n((H, N)) / np.sqrt(H) / u[:, None]).astype(np.float32),
        "unit": (np.random.uniform(0.5, 1.5, (H, 1)) * u[:, None]).astype(np.float32),
        "eps": (n((H, S)) * u[:, None]).astype(np.float32),
        "goal": ((np.random.uniform(size=(N, S)) < 0.5) * 1.0).astype(np.float32),
        "offs": striped(np.random.permutation(T)[:S]),
    }


def reference(x_words, x_scales, w1, w2, w3, unit, eps, goal, offs):
    xq = unpack_weight(x_words, x_scales)[:, unstriped(offs)]
    mu = f64(unit) * ((mxq(f64(w1), 0, "e4m3").T @ xq))
    sd = np.exp(0.3 * ((mxq(f64(w2), 0, "e4m3").T @ xq)))
    z = mu + sd * f64(eps)
    y = mxq(f64(w3), 0, "e4m3").T @ mxq(z, 0, "e4m3")
    return np.log(np.exp(y) + 1.0) - (f64(goal) * y)

@@ -1,0 +1,211 @@
+from contextlib import ExitStack
+
+import concourse.mybir as mybir
+
+K, T, S, H, N = 1024, 1024, 512, 512, 128
+FLOPS = 2 * (2 * K * H * S + H * N * S)
+
+F32 = mybir.dt.float32
+BF16 = mybir.dt.bfloat16
+I32 = mybir.dt.int32
+U32 = mybir.dt.uint32
+U16 = mybir.dt.uint16
+U8 = mybir.dt.uint8
+FP8X4 = mybir.dt.float8_e4m3fn_x4
+ACT = mybir.ActivationFunctionType
+ALU = mybir.AluOpType
+
+P = 128
+PACK = 4
+K_PASS = P * PACK
+PASSES = K // K_PASS
+HALF = S // 2
+QUADRANT = 32
+SCALE_ROWS = 4
+
+
+def tile_picked_yvae_bern_p_kernel(
+    tc, x_words, x_scales, w1, w2, w3, unit, eps, goal, offs, out
+):
+    nc = tc.nc
+    with ExitStack() as ctx:
+        sb = ctx.enter_context(tc.tile_pool(name="sb", bufs=1))
+        psum = ctx.enter_context(tc.psum_pool(name="psum", bufs=1))
+
+        def held(name, shape, dtype):
+            return sb.tile(shape, dtype, name=name, align_bytes=64)
+
+        def bank(index, name, width):
+            return psum.tile([P, width], F32, name=name, tag="bank%d" % index)
+
+        offsets = sb.tile([P, S // 16], U16, name="offsets")
+
+        one = held("one", [P, 1], F32)
+        nc.vector.memset(one[:], 1.0)
+        one_half = held("one_half", [P, 1], F32)
+        nc.scalar.activation(out=one_half[:], in_=one[:], func=ACT.Copy, scale=0.5)
+
+        scale_table = held("scale_table", [P, T], U8)
+        nc.gpsimd.memset(scale_table[:].bitcast(I32), 0)
+
+        def load_rows(name, rows):
+            raw = held(name, [P, PACK, rows.shape[1]], F32)
+            nc.sync.dma_start(out=raw[:], in_=rows.rearrange("(p j) c -> p j c", j=PACK))
+            return raw
+
+        def load_words(o):
+            table = held("word_table%d" % o, [P, T], I32)
+            nc.sync.dma_start(out=table[:], in_=x_words[o].rearrange("p n t -> p (n t)").bitcast(I32))
+            return table
+
+        def load_eps(u):
+            raw = held("eps%d" % u, [P, 2, S], F32)
+            nc.sync.dma_start(out=raw[:], in_=eps.rearrange("(p t) s -> p t s", t=PACK)[:, 2 * u : 2 * u + 2, :])
+            return raw
+
+        w2_raw = [load_rows("w2_raw0", w2[0:K_PASS, :])]
+        for q in range(P // QUADRANT):
+            nc.sync.dma_start(
+                out=scale_table[QUADRANT * q : QUADRANT * q + PASSES * SCALE_ROWS, :].bitcast(I32),
+                in_=x_scales[:, SCALE_ROWS * q : SCALE_ROWS * (q + 1), :].bitcast(I32),
+            )
+        nc.sync.dma_start(offsets[:], offs)
+        word_tables = [load_words(o) for o in range(PASSES)]
+        w2_raw.append(load_rows("w2_raw1", w2[K_PASS:K, :]))
+        w1_raw = [load_rows("w1_raw0", w1[0:K_PASS, :])]
+        eps_sb = [load_eps(u) for u in range(2)]
+        w1_raw.append(load_rows("w1_raw1", w1[K_PASS:K, :]))
+        unit_sb = held("unit_sb", [P, PACK], F32)
+        nc.sync.dma_start(out=unit_sb[:], in_=unit.rearrange("(p t) o -> p (t o)", t=PACK))
+        w3_raw = load_rows("w3_raw", w3)
+        goal_sb = held("goal_sb", [P, S], F32)
+        nc.sync.dma_start(out=goal_sb[:], in_=goal)
+
+        def group_weights(name, raw, u):
+            grouped = held(name, [P, 2, P, PACK], BF16)
+            dst = grouped[:].rearrange("p t m j -> p m j t")
+            src = raw[:].rearrange("p j (m t) -> p m j t", t=PACK)[:, :, :, 2 * u : 2 * u + 2]
+            if u == 0:
+                nc.vector.tensor_copy(out=dst, in_=src)
+            else:
+                nc.scalar.copy(out=dst, in_=src)
+            return grouped[:].rearrange("p t m j -> p (t m j)")
+
+        def quantize(name, values):
+            width = values.shape[1] // PACK
+            codes = held(name + "_codes", [P, width], U32)
+            scales = held(name + "_scales", [P, width], U8)
+            nc.vector.quantize_mx(out=codes[:].bitcast(FP8X4), scales=scales[:], in_=values)
+            return codes, scales
+
+        def quantize_pass(name, raw):
+            grouped = [group_weights("%s_bf%d" % (name, u), raw, u) for u in range(2)]
+            return [quantize("%s_q%d" % (name, u), grouped[u]) for u in range(2)]
+
+        def gather_words(o):
+            picked = held("x_codes%d" % o, [P, S], U32)
+            nc.vector.tensor_copy(out=picked[:], in_=word_tables[o][:].bitcast(U32).indirect(offsets[:]))
+            return picked
+
+        def first_product(acc, weights, t, o, cols):
+            codes, scales = weights[t // 2]
+            m = slice((t % 2) * P, (t % 2 + 1) * P)
+            nc.tensor.matmul_mx(
+                out=acc[:],
+                lhsT=codes[:, m].bitcast(FP8X4),
+                lhsT_scale=scales[:, m],
+                rhs=x_codes[o][:, cols].bitcast(FP8X4),
+                rhs_scale=x_bytes[SCALE_ROWS * o : P, cols],
+                start=(o == 0),
+                stop=(o == PASSES - 1),
+            )
+
+        halves = [slice(0, HALF), slice(HALF, S)]
+
+        w2_q = [quantize_pass("w2p0", w2_raw[0])]
+        x_codes = [gather_words(0)]
+        x_bytes = held("x_bytes", [P, S], U8)
+        nc.vector.tensor_copy(out=x_bytes[:], in_=scale_table[:].indirect(offsets[:]))
+        x_codes.append(gather_words(1))
+        log_sd = [bank(PACK + t, "log_sd%d" % t, S) for t in range(PACK)]
+        for t in range(PACK):
+            first_product(log_sd[t], w2_q[0], t, 0, slice(0, S))
+        w2_q.append(quantize_pass("w2p1", w2_raw[1]))
+        sd = held("sd", [P, PACK, S], F32)
+        for t in range(PACK):
+            first_product(log_sd[t], w2_q[1], t, 1, slice(0, S))
+            nc.scalar.activation(out=sd[:, t, :], in_=log_sd[t][:], func=ACT.Exp, scale=0.3)
+
+        w1_q = [quantize_pass("w1p0", w1_raw[0])]
+        mean = [[bank(PACK * h + t, "mean%d_%d" % (h, t), HALF) for t in range(PACK)] for h in range(2)]
+        for h in range(2):
+            for t in range(PACK):
+                first_product(mean[h][t], w1_q[0], t, 0, halves[h])
+
+        noise = held("noise", [P, PACK, S], F32)
+        for u in range(2):
+            nc.vector.tensor_tensor(
+                out=noise[:, 2 * u : 2 * u + 2, :], in0=sd[:, 2 * u : 2 * u + 2, :], in1=eps_sb[u][:], op=ALU.mult
+            )
+
+        w1_q.append(quantize_pass("w1p1", w1_raw[1]))
+        z_rows = held("z_rows", [P, PACK, HALF], BF16)
+        mu_rows = held("mu_rows", [P, PACK, HALF], F32)
+        for t in range(PACK):
+            for h in range(2):
+                first_product(mean[h][t], w1_q[1], t, 1, halves[h])
+            nc.vector.scalar_tensor_tensor(
+                out=z_rows[:, t, :], in0=mean[0][t][:], scalar=unit_sb[:, t : t + 1], in1=noise[:, t, halves[0]],
+                op0=ALU.mult, op1=ALU.add,
+            )
+            nc.scalar.activation(out=mu_rows[:, t, :], in_=mean[1][t][:], func=ACT.Copy, scale=unit_sb[:, t : t + 1])
+
+        z_grouped = [held("z_grouped%d" % h, [P, HALF, PACK], BF16) for h in range(2)]
+        nc.scalar.copy(
+            out=z_grouped[0][:].rearrange("p (c i) t -> p c t i", i=4),
+            in_=z_rows[:].rearrange("p t (c i) -> p c t i", i=4),
+        )
+        nc.vector.tensor_tensor(
+            out=z_grouped[1][:].rearrange("p (c i) t -> p c t i", i=4),
+            in0=mu_rows[:].rearrange("p t (c i) -> p c t i", i=4),
+            in1=noise[:, :, halves[1]].rearrange("p t (c i) -> p c t i", i=4),
+            op=ALU.add,
+        )
+
+        w3_grouped = held("w3_bf", [P, N, PACK], BF16)
+        nc.scalar.copy(
+            out=w3_grouped[:].rearrange("p (c i) j -> p c j i", i=4),
+            in_=w3_raw[:].rearrange("p j (c i) -> p c j i", i=4),
+        )
+        w3_codes, w3_scales = quantize("w3_q", w3_grouped[:].rearrange("p n j -> p (n j)"))
+
+        bent = held("bent", [P, S], F32)
+        ramp = held("ramp", [P, S], F32)
+        for h in range(2):
+            z_codes, z_scales = quantize("z_q%d" % h, z_grouped[h][:].rearrange("p s t -> p (s t)"))
+            y = bank(PACK * h, "y%d" % h, HALF)
+            nc.tensor.matmul_mx(
+                out=y[:],
+                lhsT=w3_codes[:].bitcast(FP8X4),
+                lhsT_scale=w3_scales[:],
+                rhs=z_codes[:].bitcast(FP8X4),
+                rhs_scale=z_scales[:],
+                start=True,
+                stop=True,
+            )
+            nc.scalar.activation(out=bent[:, halves[h]], in_=y[:], func=ACT.Tanh, scale=0.5)
+            hit = held("hit%d" % h, [P, HALF], F32)
+            nc.vector.tensor_tensor(out=hit[:], in0=y[:], in1=goal_sb[:, halves[h]], op=ALU.mult)
+            nc.vector.scalar_tensor_tensor(
+                out=ramp[:, halves[h]], in0=y[:], scalar=0.0, in1=hit[:], op0=ALU.max, op1=ALU.subtract
+            )
+        size = held("size", [P, S], F32)
+        nc.vector.scalar_tensor_tensor(
+            out=size[:], in0=bent[:], scalar=-1.0, in1=bent[:], op0=ALU.mult, op1=ALU.max
+        )
+        for h in range(2):
+            bend = held("bend%d" % h, [P, HALF], F32)
+            nc.scalar.activation(out=bend[:], in_=size[:, halves[h]], func=ACT.Ln, scale=0.5, bias=one_half[:])
+            result = held("result%d" % h, [P, HALF], F32)
+            nc.vector.tensor_tensor(out=result[:], in0=ramp[:, halves[h]], in1=bend[:], op=ALU.subtract)
+            nc.sync.dma_start(out=out[:, halves[h]], in_=result[:])

@@ -58,38 +58,41 @@ def tile_picked_yvae_bern_p_kernel(
             nc.sync.dma_start(out=table[:], in_=x_words[o].rearrange("p n t -> p (n t)").bitcast(I32))
             return table
 
-        def load_eps(u):
-            raw = held("eps%d" % u, [P, 2, S], F32)
-            nc.sync.dma_start(out=raw[:], in_=eps.rearrange("(p t) s -> p t s", t=PACK)[:, 2 * u : 2 * u + 2, :])
+        def load_eps(name, slots):
+            raw = held(name, [P, slots.stop - slots.start, S], F32)
+            nc.sync.dma_start(out=raw[:], in_=eps.rearrange("(p t) s -> p t s", t=PACK)[:, slots, :])
             return raw
 
-        w2_raw = [load_rows("w2_raw0", w2[0:K_PASS, :])]
+        eps_slots = [slice(0, 2), slice(2, 4)]
+        nc.sync.dma_start(offsets[:], offs)
+        word_tables = [load_words(0)]
         for q in range(P // QUADRANT):
             nc.sync.dma_start(
                 out=scale_table[QUADRANT * q : QUADRANT * q + PASSES * SCALE_ROWS, :].bitcast(I32),
                 in_=x_scales[:, SCALE_ROWS * q : SCALE_ROWS * (q + 1), :].bitcast(I32),
             )
-        nc.sync.dma_start(offsets[:], offs)
-        word_tables = [load_words(o) for o in range(PASSES)]
+        w2_raw = [load_rows("w2_raw0", w2[0:K_PASS, :])]
+        word_tables.append(load_words(1))
         w2_raw.append(load_rows("w2_raw1", w2[K_PASS:K, :]))
         w1_raw = [load_rows("w1_raw0", w1[0:K_PASS, :])]
-        eps_sb = [load_eps(u) for u in range(2)]
-        w1_raw.append(load_rows("w1_raw1", w1[K_PASS:K, :]))
+        eps_sb = [load_eps("eps0", eps_slots[0])]
+        w1_last = [load_rows("w1_raw1_%d" % c, w1[K_PASS:K, c * H // 2 : (c + 1) * H // 2]) for c in range(2)]
         unit_sb = held("unit_sb", [P, PACK], F32)
         nc.sync.dma_start(out=unit_sb[:], in_=unit.rearrange("(p t) o -> p (t o)", t=PACK))
+        eps_sb.append(load_eps("eps1", eps_slots[1]))
         w3_raw = load_rows("w3_raw", w3)
         goal_sb = held("goal_sb", [P, S], F32)
         nc.sync.dma_start(out=goal_sb[:], in_=goal)
 
-        def group_weights(name, raw, u):
-            grouped = held(name, [P, 2, P, PACK], BF16)
-            dst = grouped[:].rearrange("p t m j -> p m j t")
-            src = raw[:].rearrange("p j (m t) -> p m j t", t=PACK)[:, :, :, 2 * u : 2 * u + 2]
-            if u == 0:
-                nc.vector.tensor_copy(out=dst, in_=src)
-            else:
-                nc.scalar.copy(out=dst, in_=src)
-            return grouped[:].rearrange("p t m j -> p (t m j)")
+        def group_weights(copy, grouped, raw, u, first_m):
+            count = raw.shape[2] // PACK
+            copy(
+                out=grouped[:, :, first_m : first_m + count, :].rearrange("p t m j -> p m j t"),
+                in_=raw[:].rearrange("p j (m t) -> p m j t", t=PACK)[:, :, :, 2 * u : 2 * u + 2],
+            )
+
+        def grouped_pair(name):
+            return [held("%s_bf%d" % (name, u), [P, 2, P, PACK], BF16) for u in range(2)]
 
         def quantize(name, values):
             width = values.shape[1] // PACK
@@ -98,9 +101,14 @@ def tile_picked_yvae_bern_p_kernel(
             nc.vector.quantize_mx(out=codes[:].bitcast(FP8X4), scales=scales[:], in_=values)
             return codes, scales
 
+        def quantize_pair(name, grouped):
+            return [quantize("%s_q%d" % (name, u), grouped[u][:].rearrange("p t m j -> p (t m j)")) for u in range(2)]
+
         def quantize_pass(name, raw):
-            grouped = [group_weights("%s_bf%d" % (name, u), raw, u) for u in range(2)]
-            return [quantize("%s_q%d" % (name, u), grouped[u]) for u in range(2)]
+            grouped = grouped_pair(name)
+            group_weights(nc.vector.tensor_copy, grouped[0], raw, 0, 0)
+            group_weights(nc.scalar.copy, grouped[1], raw, 1, 0)
+            return quantize_pair(name, grouped)
 
         def gather_words(o):
             picked = held("x_codes%d" % o, [P, S], U32)
@@ -122,55 +130,58 @@ def tile_picked_yvae_bern_p_kernel(
 
         halves = [slice(0, HALF), slice(HALF, S)]
 
-        w2_q = [quantize_pass("w2p0", w2_raw[0])]
         x_codes = [gather_words(0)]
         x_bytes = held("x_bytes", [P, S], U8)
         nc.vector.tensor_copy(out=x_bytes[:], in_=scale_table[:].indirect(offsets[:]))
+        w2_q = [quantize_pass("w2p0", w2_raw[0])]
         x_codes.append(gather_words(1))
         log_sd = [bank(PACK + t, "log_sd%d" % t, S) for t in range(PACK)]
         for t in range(PACK):
             first_product(log_sd[t], w2_q[0], t, 0, slice(0, S))
         w2_q.append(quantize_pass("w2p1", w2_raw[1]))
-        sd = held("sd", [P, PACK, S], F32)
         for t in range(PACK):
             first_product(log_sd[t], w2_q[1], t, 1, slice(0, S))
+
+        sd = held("sd", [P, PACK, S], F32)
+        noise = held("noise", [P, PACK, S], F32)
+
+        def deviation(t):
             nc.scalar.activation(out=sd[:, t, :], in_=log_sd[t][:], func=ACT.Exp, scale=0.3)
 
+        def scale_noise(u, cols):
+            nc.vector.tensor_tensor(
+                out=noise[:, eps_slots[u], cols], in0=sd[:, eps_slots[u], cols], in1=eps_sb[u][:, :, cols], op=ALU.mult
+            )
+
+        deviation(0)
+        deviation(1)
         w1_q = [quantize_pass("w1p0", w1_raw[0])]
+        deviation(2)
+        deviation(3)
         mean = [[bank(PACK * h + t, "mean%d_%d" % (h, t), HALF) for t in range(PACK)] for h in range(2)]
         for h in range(2):
             for t in range(PACK):
                 first_product(mean[h][t], w1_q[0], t, 0, halves[h])
+        scale_noise(0, slice(0, S))
 
-        noise = held("noise", [P, PACK, S], F32)
+        grouped = grouped_pair("w1p1")
         for u in range(2):
-            nc.vector.tensor_tensor(
-                out=noise[:, 2 * u : 2 * u + 2, :], in0=sd[:, 2 * u : 2 * u + 2, :], in1=eps_sb[u][:], op=ALU.mult
-            )
-
-        w1_q.append(quantize_pass("w1p1", w1_raw[1]))
+            group_weights(nc.vector.tensor_copy, grouped[u], w1_last[0], u, 0)
+        group_weights(nc.vector.tensor_copy, grouped[0], w1_last[1], 0, P // 2)
+        group_weights(nc.scalar.copy, grouped[1], w1_last[1], 1, P // 2)
+        w1_q.append(quantize_pair("w1p1", grouped))
+        scale_noise(1, halves[0])
         z_rows = held("z_rows", [P, PACK, HALF], BF16)
         mu_rows = held("mu_rows", [P, PACK, HALF], F32)
         for t in range(PACK):
-            for h in range(2):
+            for h in (1, 0):
                 first_product(mean[h][t], w1_q[1], t, 1, halves[h])
+            nc.scalar.activation(out=mu_rows[:, t, :], in_=mean[1][t][:], func=ACT.Copy, scale=unit_sb[:, t : t + 1])
             nc.vector.scalar_tensor_tensor(
                 out=z_rows[:, t, :], in0=mean[0][t][:], scalar=unit_sb[:, t : t + 1], in1=noise[:, t, halves[0]],
                 op0=ALU.mult, op1=ALU.add,
             )
-            nc.scalar.activation(out=mu_rows[:, t, :], in_=mean[1][t][:], func=ACT.Copy, scale=unit_sb[:, t : t + 1])
-
-        z_grouped = [held("z_grouped%d" % h, [P, HALF, PACK], BF16) for h in range(2)]
-        nc.scalar.copy(
-            out=z_grouped[0][:].rearrange("p (c i) t -> p c t i", i=4),
-            in_=z_rows[:].rearrange("p t (c i) -> p c t i", i=4),
-        )
-        nc.vector.tensor_tensor(
-            out=z_grouped[1][:].rearrange("p (c i) t -> p c t i", i=4),
-            in0=mu_rows[:].rearrange("p t (c i) -> p c t i", i=4),
-            in1=noise[:, :, halves[1]].rearrange("p t (c i) -> p c t i", i=4),
-            op=ALU.add,
-        )
+        scale_noise(1, halves[1])
 
         w3_grouped = held("w3_bf", [P, N, PACK], BF16)
         nc.scalar.copy(
@@ -179,13 +190,31 @@ def tile_picked_yvae_bern_p_kernel(
         )
         w3_codes, w3_scales = quantize("w3_q", w3_grouped[:].rearrange("p n j -> p (n j)"))
 
+        chunks = [slice(0, HALF), slice(HALF, HALF + HALF // 2), slice(HALF + HALF // 2, S)]
+        z_grouped = [held("z_grouped%d" % c, [P, cols.stop - cols.start, PACK], BF16) for c, cols in enumerate(chunks)]
+        nc.scalar.copy(
+            out=z_grouped[0][:].rearrange("p (c i) t -> p c t i", i=4),
+            in_=z_rows[:].rearrange("p t (c i) -> p c t i", i=4),
+        )
+
+        def add_noise(c):
+            cols = chunks[c]
+            nc.vector.tensor_tensor(
+                out=z_grouped[c][:].rearrange("p (c i) t -> p c t i", i=4),
+                in0=mu_rows[:, :, cols.start - HALF : cols.stop - HALF].rearrange("p t (c i) -> p c t i", i=4),
+                in1=noise[:, :, cols].rearrange("p t (c i) -> p c t i", i=4),
+                op=ALU.add,
+            )
+
+        ys = []
         bent = held("bent", [P, S], F32)
-        ramp = held("ramp", [P, S], F32)
-        for h in range(2):
-            z_codes, z_scales = quantize("z_q%d" % h, z_grouped[h][:].rearrange("p s t -> p (s t)"))
-            y = bank(PACK * h, "y%d" % h, HALF)
+
+        def decode(c):
+            cols = chunks[c]
+            z_codes, z_scales = quantize("z_q%d" % c, z_grouped[c][:].rearrange("p s t -> p (s t)"))
+            ys.append(bank(c, "y%d" % c, cols.stop - cols.start))
             nc.tensor.matmul_mx(
-                out=y[:],
+                out=ys[c][:],
                 lhsT=w3_codes[:].bitcast(FP8X4),
                 lhsT_scale=w3_scales[:],
                 rhs=z_codes[:].bitcast(FP8X4),
@@ -193,16 +222,25 @@ def tile_picked_yvae_bern_p_kernel(
                 start=True,
                 stop=True,
             )
-            nc.scalar.activation(out=bent[:, halves[h]], in_=y[:], func=ACT.Tanh, scale=0.5)
-            hit = held("hit%d" % h, [P, HALF], F32)
-            nc.vector.tensor_tensor(out=hit[:], in0=y[:], in1=goal_sb[:, halves[h]], op=ALU.mult)
-            nc.vector.scalar_tensor_tensor(
-                out=ramp[:, halves[h]], in0=y[:], scalar=0.0, in1=hit[:], op0=ALU.max, op1=ALU.subtract
-            )
+            nc.scalar.activation(out=bent[:, cols], in_=ys[c][:], func=ACT.Tanh, scale=0.5)
+
+        add_noise(1)
+        decode(0)
+        add_noise(2)
+        decode(1)
+        decode(2)
+
         size = held("size", [P, S], F32)
         nc.vector.scalar_tensor_tensor(
             out=size[:], in0=bent[:], scalar=-1.0, in1=bent[:], op0=ALU.mult, op1=ALU.max
         )
+        ramp = held("ramp", [P, S], F32)
+        for c, cols in enumerate(chunks):
+            hit = held("hit%d" % c, [P, cols.stop - cols.start], F32)
+            nc.vector.tensor_tensor(out=hit[:], in0=ys[c][:], in1=goal_sb[:, cols], op=ALU.mult)
+            nc.vector.scalar_tensor_tensor(
+                out=ramp[:, cols], in0=ys[c][:], scalar=0.0, in1=hit[:], op0=ALU.max, op1=ALU.subtract
+            )
         for h in range(2):
             bend = held("bend%d" % h, [P, HALF], F32)
             nc.scalar.activation(out=bend[:], in_=size[:, halves[h]], func=ACT.Ln, scale=0.5, bias=one_half[:])

from contextlib import ExitStack

import concourse.mybir as mybir

K, T, S, H, N = 1024, 1024, 512, 512, 128
FLOPS = 2 * (2 * K * H * S + H * N * S)

F32 = mybir.dt.float32
BF16 = mybir.dt.bfloat16
I32 = mybir.dt.int32
U32 = mybir.dt.uint32
U16 = mybir.dt.uint16
U8 = mybir.dt.uint8
FP8X4 = mybir.dt.float8_e4m3fn_x4
ACT = mybir.ActivationFunctionType
ALU = mybir.AluOpType

P = 128
PACK = 4
K_PASS = P * PACK
PASSES = K // K_PASS
HALF = S // 2
QUADRANT = 32
SCALE_ROWS = 4


def tile_picked_yvae_bern_p_kernel(
    tc, x_words, x_scales, w1, w2, w3, unit, eps, goal, offs, out
):
    nc = tc.nc
    with ExitStack() as ctx:
        sb = ctx.enter_context(tc.tile_pool(name="sb", bufs=1))
        psum = ctx.enter_context(tc.psum_pool(name="psum", bufs=1))

        def held(name, shape, dtype):
            return sb.tile(shape, dtype, name=name, align_bytes=64)

        def bank(index, name, width):
            return psum.tile([P, width], F32, name=name, tag="bank%d" % index)

        offsets = sb.tile([P, S // 16], U16, name="offsets")

        one = held("one", [P, 1], F32)
        nc.vector.memset(one[:], 1.0)
        one_half = held("one_half", [P, 1], F32)
        nc.scalar.activation(out=one_half[:], in_=one[:], func=ACT.Copy, scale=0.5)

        scale_table = held("scale_table", [P, T], U8)
        nc.gpsimd.memset(scale_table[:].bitcast(I32), 0)

        def load_rows(name, rows):
            raw = held(name, [P, PACK, rows.shape[1]], F32)
            nc.sync.dma_start(out=raw[:], in_=rows.rearrange("(p j) c -> p j c", j=PACK))
            return raw

        def load_words(o):
            table = held("word_table%d" % o, [P, T], I32)
            nc.sync.dma_start(out=table[:], in_=x_words[o].rearrange("p n t -> p (n t)").bitcast(I32))
            return table

        def load_eps(name, slots):
            raw = held(name, [P, slots.stop - slots.start, S], F32)
            nc.sync.dma_start(out=raw[:], in_=eps.rearrange("(p t) s -> p t s", t=PACK)[:, slots, :])
            return raw

        eps_slots = [slice(0, 2), slice(2, 4)]
        nc.sync.dma_start(offsets[:], offs)
        word_tables = [load_words(0)]
        for q in range(P // QUADRANT):
            nc.sync.dma_start(
                out=scale_table[QUADRANT * q : QUADRANT * q + PASSES * SCALE_ROWS, :].bitcast(I32),
                in_=x_scales[:, SCALE_ROWS * q : SCALE_ROWS * (q + 1), :].bitcast(I32),
            )
        w2_raw = [load_rows("w2_raw0", w2[0:K_PASS, :])]
        word_tables.append(load_words(1))
        w2_raw.append(load_rows("w2_raw1", w2[K_PASS:K, :]))
        w1_raw = [load_rows("w1_raw0", w1[0:K_PASS, :])]
        eps_sb = [load_eps("eps0", eps_slots[0])]
        w1_last = [load_rows("w1_raw1_%d" % c, w1[K_PASS:K, c * H // 2 : (c + 1) * H // 2]) for c in range(2)]
        unit_sb = held("unit_sb", [P, PACK], F32)
        nc.sync.dma_start(out=unit_sb[:], in_=unit.rearrange("(p t) o -> p (t o)", t=PACK))
        eps_sb.append(load_eps("eps1", eps_slots[1]))
        w3_raw = load_rows("w3_raw", w3)
        goal_sb = held("goal_sb", [P, S], F32)
        nc.sync.dma_start(out=goal_sb[:], in_=goal)

        def group_weights(copy, grouped, raw, u, first_m):
            count = raw.shape[2] // PACK
            copy(
                out=grouped[:, :, first_m : first_m + count, :].rearrange("p t m j -> p m j t"),
                in_=raw[:].rearrange("p j (m t) -> p m j t", t=PACK)[:, :, :, 2 * u : 2 * u + 2],
            )

        def grouped_pair(name):
            return [held("%s_bf%d" % (name, u), [P, 2, P, PACK], BF16) for u in range(2)]

        def quantize(name, values):
            width = values.shape[1] // PACK
            codes = held(name + "_codes", [P, width], U32)
            scales = held(name + "_scales", [P, width], U8)
            nc.vector.quantize_mx(out=codes[:].bitcast(FP8X4), scales=scales[:], in_=values)
            return codes, scales

        def quantize_pair(name, grouped):
            return [quantize("%s_q%d" % (name, u), grouped[u][:].rearrange("p t m j -> p (t m j)")) for u in range(2)]

        def quantize_pass(name, raw):
            grouped = grouped_pair(name)
            group_weights(nc.vector.tensor_copy, grouped[0], raw, 0, 0)
            group_weights(nc.scalar.copy, grouped[1], raw, 1, 0)
            return quantize_pair(name, grouped)

        def gather_words(o):
            picked = held("x_codes%d" % o, [P, S], U32)
            nc.vector.tensor_copy(out=picked[:], in_=word_tables[o][:].bitcast(U32).indirect(offsets[:]))
            return picked

        def first_product(acc, weights, t, o, cols):
            codes, scales = weights[t // 2]
            m = slice((t % 2) * P, (t % 2 + 1) * P)
            nc.tensor.matmul_mx(
                out=acc[:],
                lhsT=codes[:, m].bitcast(FP8X4),
                lhsT_scale=scales[:, m],
                rhs=x_codes[o][:, cols].bitcast(FP8X4),
                rhs_scale=x_bytes[SCALE_ROWS * o : P, cols],
                start=(o == 0),
                stop=(o == PASSES - 1),
            )

        halves = [slice(0, HALF), slice(HALF, S)]

        x_codes = [gather_words(0)]
        x_bytes = held("x_bytes", [P, S], U8)
        nc.vector.tensor_copy(out=x_bytes[:], in_=scale_table[:].indirect(offsets[:]))
        w2_q = [quantize_pass("w2p0", w2_raw[0])]
        x_codes.append(gather_words(1))
        log_sd = [bank(PACK + t, "log_sd%d" % t, S) for t in range(PACK)]
        for t in range(PACK):
            first_product(log_sd[t], w2_q[0], t, 0, slice(0, S))
        w2_q.append(quantize_pass("w2p1", w2_raw[1]))
        for t in range(PACK):
            first_product(log_sd[t], w2_q[1], t, 1, slice(0, S))

        sd = held("sd", [P, PACK, S], F32)
        noise = held("noise", [P, PACK, S], F32)

        def deviation(t):
            nc.scalar.activation(out=sd[:, t, :], in_=log_sd[t][:], func=ACT.Exp, scale=0.3)

        def scale_noise(u, cols):
            nc.vector.tensor_tensor(
                out=noise[:, eps_slots[u], cols], in0=sd[:, eps_slots[u], cols], in1=eps_sb[u][:, :, cols], op=ALU.mult
            )

        deviation(0)
        deviation(1)
        w1_q = [quantize_pass("w1p0", w1_raw[0])]
        deviation(2)
        deviation(3)
        mean = [[bank(PACK * h + t, "mean%d_%d" % (h, t), HALF) for t in range(PACK)] for h in range(2)]
        for h in range(2):
            for t in range(PACK):
                first_product(mean[h][t], w1_q[0], t, 0, halves[h])
        scale_noise(0, slice(0, S))

        grouped = grouped_pair("w1p1")
        for u in range(2):
            group_weights(nc.vector.tensor_copy, grouped[u], w1_last[0], u, 0)
        group_weights(nc.vector.tensor_copy, grouped[0], w1_last[1], 0, P // 2)
        group_weights(nc.scalar.copy, grouped[1], w1_last[1], 1, P // 2)
        w1_q.append(quantize_pair("w1p1", grouped))
        scale_noise(1, halves[0])
        z_rows = held("z_rows", [P, PACK, HALF], BF16)
        mu_rows = held("mu_rows", [P, PACK, HALF], F32)
        for t in range(PACK):
            for h in (1, 0):
                first_product(mean[h][t], w1_q[1], t, 1, halves[h])
            nc.scalar.activation(out=mu_rows[:, t, :], in_=mean[1][t][:], func=ACT.Copy, scale=unit_sb[:, t : t + 1])
            nc.vector.scalar_tensor_tensor(
                out=z_rows[:, t, :], in0=mean[0][t][:], scalar=unit_sb[:, t : t + 1], in1=noise[:, t, halves[0]],
                op0=ALU.mult, op1=ALU.add,
            )
        scale_noise(1, halves[1])

        w3_grouped = held("w3_bf", [P, N, PACK], BF16)
        nc.scalar.copy(
            out=w3_grouped[:].rearrange("p (c i) j -> p c j i", i=4),
            in_=w3_raw[:].rearrange("p j (c i) -> p c j i", i=4),
        )
        w3_codes, w3_scales = quantize("w3_q", w3_grouped[:].rearrange("p n j -> p (n j)"))

        chunks = [slice(0, HALF), slice(HALF, HALF + HALF // 2), slice(HALF + HALF // 2, S)]
        z_grouped = [held("z_grouped%d" % c, [P, cols.stop - cols.start, PACK], BF16) for c, cols in enumerate(chunks)]
        nc.scalar.copy(
            out=z_grouped[0][:].rearrange("p (c i) t -> p c t i", i=4),
            in_=z_rows[:].rearrange("p t (c i) -> p c t i", i=4),
        )

        def add_noise(c):
            cols = chunks[c]
            nc.vector.tensor_tensor(
                out=z_grouped[c][:].rearrange("p (c i) t -> p c t i", i=4),
                in0=mu_rows[:, :, cols.start - HALF : cols.stop - HALF].rearrange("p t (c i) -> p c t i", i=4),
                in1=noise[:, :, cols].rearrange("p t (c i) -> p c t i", i=4),
                op=ALU.add,
            )

        ys = []
        bent = held("bent", [P, S], F32)

        def decode(c):
            cols = chunks[c]
            z_codes, z_scales = quantize("z_q%d" % c, z_grouped[c][:].rearrange("p s t -> p (s t)"))
            ys.append(bank(c, "y%d" % c, cols.stop - cols.start))
            nc.tensor.matmul_mx(
                out=ys[c][:],
                lhsT=w3_codes[:].bitcast(FP8X4),
                lhsT_scale=w3_scales[:],
                rhs=z_codes[:].bitcast(FP8X4),
                rhs_scale=z_scales[:],
                start=True,
                stop=True,
            )
            nc.scalar.activation(out=bent[:, cols], in_=ys[c][:], func=ACT.Tanh, scale=0.5)

        add_noise(1)
        decode(0)
        add_noise(2)
        decode(1)
        decode(2)

        size = held("size", [P, S], F32)
        nc.vector.scalar_tensor_tensor(
            out=size[:], in0=bent[:], scalar=-1.0, in1=bent[:], op0=ALU.mult, op1=ALU.max
        )
        ramp = held("ramp", [P, S], F32)
        for c, cols in enumerate(chunks):
            hit = held("hit%d" % c, [P, cols.stop - cols.start], F32)
            nc.vector.tensor_tensor(out=hit[:], in0=ys[c][:], in1=goal_sb[:, cols], op=ALU.mult)
            nc.vector.scalar_tensor_tensor(
                out=ramp[:, cols], in0=ys[c][:], scalar=0.0, in1=hit[:], op0=ALU.max, op1=ALU.subtract
            )
        for h in range(2):
            bend = held("bend%d" % h, [P, HALF], F32)
            nc.scalar.activation(out=bend[:], in_=size[:, halves[h]], func=ACT.Ln, scale=0.5, bias=one_half[:])
            result = held("result%d" % h, [P, HALF], F32)
            nc.vector.tensor_tensor(out=result[:], in0=ramp[:, halves[h]], in1=bend[:], op=ALU.subtract)
            nc.sync.dma_start(out=out[:, halves[h]], in_=result[:])
